import numpy as np
import ml_dtypes


def mxq(x, axis, fmt="e4m3"):
    dtype, down = {"e4m3": (ml_dtypes.float8_e4m3fn, 7), "e5m2": (ml_dtypes.float8_e5m2, 14)}[fmt]
    v = np.moveaxis(np.asarray(x, np.float32).astype(ml_dtypes.bfloat16).astype(np.float64), axis, -1)
    blocks = v.reshape(v.shape[:-1] + (-1, 32))
    amax = np.abs(blocks).max(-1, keepdims=True)
    byte = np.maximum(np.where(amax > 0, np.frexp(amax)[1] - 1 + 127, 0) - down, 1)
    scale = np.exp2(byte - 127.0)
    codes = (blocks / scale).astype(np.float32).astype(dtype).astype(np.float64)
    return np.moveaxis((codes * scale).reshape(v.shape), -1, axis)


WIDE = False


def mx_kscale(k):
    if not WIDE:
        return np.ones(k)
    levels = np.array([10, -10, 5, -5, 0])
    if k % 512:
        return np.exp2(np.random.permutation(np.resize(levels, k // 32))).repeat(32)
    a = np.empty((k // 512, 16))
    for p in range(k // 512):
        a[p, :8] = np.random.permutation(np.resize(levels, 8))
        for g in range(8):
            far = levels[np.abs(levels - a[p, g]) >= 10]
            a[p, g + 8] = far[np.random.randint(len(far))]
    return np.exp2(a.ravel()).repeat(32)


def f64(x):
    return np.asarray(x).astype(np.float64)


def striped8(idx):
    return np.asarray(idx).reshape(8, -1, 16).transpose(0, 2, 1).reshape(128, -1).astype(np.uint16)


def unstriped8(offs):
    return offs.reshape(8, 16, -1).transpose(0, 2, 1).reshape(8, -1).astype(np.int64)


def pick8(x, idx, run):
    r = np.arange(len(x))
    return x[r[:, None], idx[r % (8 * run) // run]]


E2M1 = np.array([0.0, 0.5, 1.0, 1.5, 2.0, 3.0, 4.0, 6.0, -0.0, -0.5, -1.0, -1.5, -2.0, -3.0, -4.0, -6.0])


def pack_weight(w, fmt):
    k, n = w.shape
    w = f64(np.asarray(w, np.float32).astype(ml_dtypes.bfloat16)).reshape(k // 32, 32, n)
    amax = np.abs(w).max(1)
    if fmt == "e4m3":
        byte = np.frexp(amax)[1] - 1 + 127 - 7
    else:
        mant, ex = np.frexp(amax / 6.0)
        byte = np.where(mant > 0.5, ex, ex - 1) + 127
    byte = np.clip(np.where(amax > 0, byte, 1), 1, 254)
    scaled = (w * np.exp2(127.0 - byte)[:, None, :]).reshape(k, n).astype(np.float32)
    by_word = np.ascontiguousarray(scaled.reshape(k // 512, 128, 4, n).transpose(0, 1, 3, 2))
    if fmt == "e4m3":
        words = by_word.astype(ml_dtypes.float8_e4m3fn).view(np.uint8)
    else:
        c = by_word.astype(ml_dtypes.float4_e2m1fn).view(np.uint8) & 0xF
        words = (c[..., 0::2] | (c[..., 1::2] << 4)).reshape(k // 512, 128, 2 * n)
    return np.ascontiguousarray(words), np.ascontiguousarray(byte.astype(np.uint8).reshape(k // 512, 16, n))


def unpack_weight(words, scales, fmt):
    g, _, n = scales.shape
    words = np.ascontiguousarray(words).reshape(g, 128, n, -1)
    if fmt == "e4m3":
        vals = words.view(ml_dtypes.float8_e4m3fn).astype(np.float64)
    else:
        nib = np.empty((g, 128, n, 4), np.uint8)
        nib[..., 0::2] = words & 0xF
        nib[..., 1::2] = words >> 4
        vals = E2M1[nib]
    vals = vals * np.repeat(np.exp2(scales.astype(np.float64) - 127.0), 8, axis=1)[..., None]
    return vals.transpose(0, 1, 3, 2).reshape(g * 512, n)


D, T, I, Q = 512, 1024, 512, 128


def setup_inputs():
    n = np.random.standard_normal
    idx = np.stack([np.random.permutation(T)[:I] for _ in range(8)])
    idx2 = np.stack([np.random.permutation(T)[:I] for _ in range(8)])
    idx3 = np.stack([np.random.permutation(T)[:I] for _ in range(8)])
    idx4 = np.stack([np.random.permutation(T)[:I] for _ in range(8)])
    fd = mx_kscale(D)
    keysp = pack_weight(n((D, T)) / fd[:, None], "e4m3")
    return {
        "query": (n((D, Q)) * 1.0 / np.sqrt(D) * fd[:, None]).astype(np.float32),
        "keys_words": keysp[0],
        "keys_scales": keysp[1],
        "old": (np.random.uniform(0.3, 1.7, (Q, T))).astype(np.float32),
        "base": (0.5 * n((Q, T))).astype(np.float32),
        "offs": striped8(idx),
        "offs2": striped8(idx2),
        "offs3": striped8(idx3),
        "offs4": striped8(idx4),
    }


def reference(query, keys_words, keys_scales, old, base, offs, offs2, offs3, offs4):
    idx = unstriped8(offs)
    idx2 = unstriped8(offs2)
    idx3 = unstriped8(offs3)
    idx4 = unstriped8(offs4)
    keysu = unpack_weight(keys_words, keys_scales, "e4m3")
    queryq = mxq(f64(query), 0, "e4m3")
    a = queryq.T @ keysu
    s = pick8(a, idx, 16) - pick8(a, idx2, 16)
    w = np.maximum(s, 0.0)
    ws = w * pick8(f64(old), idx3, 16)
    f1 = np.zeros((Q, T))
    f1[np.arange(Q)[:, None], idx4[np.arange(Q) % 128 // 16]] = ws
    y = f64(base) + f1
    return y

@@ -1,0 +1,116 @@
+from contextlib import ExitStack
+
+import concourse.mybir as mybir
+
+D, T, SLOTS, Q = 512, 1024, 512, 128
+FLOPS = 2 * D * Q * T
+
+F32 = mybir.dt.float32
+BF16 = mybir.dt.bfloat16
+I32 = mybir.dt.int32
+U32 = mybir.dt.uint32
+U16 = mybir.dt.uint16
+U8 = mybir.dt.uint8
+FP8X4 = mybir.dt.float8_e4m3fn_x4
+ALU = mybir.AluOpType
+ACT = mybir.ActivationFunctionType
+
+P = 128
+PACK = 4
+QUARTERS = 4
+N = T // QUARTERS
+HALF = SLOTS // 2
+PER_COLUMN = 16
+
+
+def tile_attend_difference_lean_timesold_heads_kernel(tc, query, keys_words, keys_scales, old, base, offs, offs2, offs3, offs4, out):
+    nc = tc.nc
+    with ExitStack() as ctx:
+        pool = ctx.enter_context(tc.tile_pool(name="pool", bufs=1))
+        psum = ctx.enter_context(tc.psum_pool(name="psum", bufs=1))
+
+        key_scales = pool.tile([P, N], U8, name="key_scales", align_bytes=64)
+        nc.gpsimd.memset(key_scales[:].bitcast(U32), 0)
+
+        query_rows = pool.tile([P, PACK, Q], F32, name="query_rows")
+        nc.sync.dma_start(query_rows[:], query.rearrange("(p j) q -> p j q", j=PACK))
+
+        scale_rows = keys_scales[0].bitcast(I32)
+        for quadrant in range(4):
+            nc.sync.dma_start(
+                key_scales[:].bitcast(I32)[32 * quadrant : 32 * quadrant + 16, :],
+                scale_rows[4 * quadrant : 4 * quadrant + 4, :].rearrange("r (j c) -> j r c", j=QUARTERS),
+            )
+
+        key_words = pool.tile([P, T], U32, name="key_words", align_bytes=64)
+        word_rows = keys_words[0].rearrange("p n t -> p (n t)").bitcast(I32)
+        for h in range(2):
+            tokens = slice(h * T // 2, (h + 1) * T // 2)
+            nc.sync.dma_start(key_words[:].bitcast(I32)[:, tokens], word_rows[:, tokens])
+
+        def load_list(name, source):
+            offsets = pool.tile([P, SLOTS // PER_COLUMN], U16, name=name)
+            nc.sync.dma_start(offsets[:], source)
+            return offsets
+
+        list2 = load_list("list2", offs2)
+        list1 = load_list("list1", offs)
+        old_table = pool.tile([P, T], F32, name="old_table")
+        nc.sync.dma_start(old_table[:], old)
+        list3 = load_list("list3", offs3)
+        list4 = load_list("list4", offs4)
+        base_table = pool.tile([P, T], F32, name="base_table")
+        nc.sync.dma_start(base_table[:], base)
+
+        placed = pool.tile([P, T], F32, name="placed")
+        nc.vector.memset(placed[:], 0.0)
+
+        query_bf16 = pool.tile([P, Q, PACK], BF16, name="query_bf16", align_bytes=64)
+        for h, copy in enumerate((nc.vector.tensor_copy, nc.scalar.copy)):
+            rows = slice(h * Q // 2, (h + 1) * Q // 2)
+            copy(
+                query_bf16[:, rows, :].rearrange("p (c i) j -> p c j i", i=4),
+                query_rows[:, :, rows].rearrange("p j (c i) -> p c j i", i=4),
+            )
+        query_codes = pool.tile([P, Q], U32, name="query_codes", align_bytes=64)
+        query_scales = pool.tile([P, Q], U8, name="query_scales", align_bytes=64)
+        nc.vector.quantize_mx(query_codes[:].bitcast(FP8X4), query_scales[:], query_bf16[:].rearrange("p q j -> p (q j)"))
+
+        products = pool.tile([P, T], F32, name="products", tag="products_then_old_listed")
+        for j in range(QUARTERS):
+            tokens = slice(j * N, (j + 1) * N)
+            bank = psum.tile([P, N], F32, name=f"bank{j}")
+            nc.tensor.matmul_mx(
+                bank[:],
+                lhsT=query_codes[:].bitcast(FP8X4),
+                lhsT_scale=query_scales[:],
+                rhs=key_words[:, tokens].bitcast(FP8X4),
+                rhs_scale=key_scales[4 * j : P, :],
+                start=True,
+                stop=True,
+            )
+            if j % 2 == 0:
+                nc.scalar.copy(products[:, tokens], bank[:])
+            else:
+                nc.vector.tensor_copy(products[:, tokens], bank[:])
+
+        first = pool.tile([P, SLOTS], F32, name="first")
+        second = pool.tile([P, SLOTS], F32, name="second")
+        scores = pool.tile([P, SLOTS], F32, name="scores")
+        weights = pool.tile([P, SLOTS], F32, name="weights")
+        nc.scalar.activation(second[:], products[:].indirect(list2[:]), ACT.Copy)
+        nc.vector.tensor_copy(first[:], products[:].indirect(list1[:]))
+        old_listed = pool.tile([P, SLOTS], F32, name="old_listed", tag="products_then_old_listed")
+        nc.scalar.activation(old_listed[:], old_table[:].indirect(list3[:]), ACT.Copy)
+        halves = [slice(h * HALF, (h + 1) * HALF) for h in range(2)]
+        for slots in halves:
+            nc.vector.tensor_tensor(scores[:, slots], first[:, slots], second[:, slots], ALU.subtract)
+        for slots in halves:
+            nc.vector.tensor_scalar_max(weights[:, slots], scores[:, slots], 0.0)
+        nc.vector.tensor_tensor(placed[:].indirect(list4[:]), weights[:], old_listed[:], ALU.mult)
+
+        result = pool.tile([P, T], F32, name="result")
+        for j, queue in enumerate((nc.sync, nc.scalar, nc.sync, nc.scalar)):
+            tokens = slice(j * N, (j + 1) * N)
+            nc.vector.tensor_tensor(result[:, tokens], placed[:, tokens], base_table[:, tokens], ALU.add)
+            queue.dma_start(out[:, tokens], result[:, tokens])

@@ -30,7 +30,7 @@ def tile_attend_difference_lean_timesold_heads_kernel(tc, query, keys_words, key
         psum = ctx.enter_context(tc.psum_pool(name="psum", bufs=1))
 
         key_scales = pool.tile([P, N], U8, name="key_scales", align_bytes=64)
-        nc.gpsimd.memset(key_scales[:].bitcast(U32), 0)
+        nc.vector.memset(key_scales[:].bitcast(U32), 0)
 
         query_rows = pool.tile([P, PACK, Q], F32, name="query_rows")
         nc.sync.dma_start(query_rows[:], query.rearrange("(p j) q -> p j q", j=PACK))
@@ -76,33 +76,38 @@ def tile_attend_difference_lean_timesold_heads_kernel(tc, query, keys_words, key
         query_scales = pool.tile([P, Q], U8, name="query_scales", align_bytes=64)
         nc.vector.quantize_mx(query_codes[:].bitcast(FP8X4), query_scales[:], query_bf16[:].rearrange("p q j -> p (q j)"))
 
-        products = pool.tile([P, T], F32, name="products", tag="products_then_old_listed")
-        for j in range(QUARTERS):
-            tokens = slice(j * N, (j + 1) * N)
-            bank = psum.tile([P, N], F32, name=f"bank{j}")
+        products = pool.tile([P, T], F32, name="products")
+        starts = [0, N, 2 * N, 3 * N, 3 * N + N // 2, T]
+        for i in range(len(starts) - 1):
+            tokens = slice(starts[i], starts[i + 1])
+            j = tokens.start // N
+            bank = psum.tile([P, tokens.stop - tokens.start], F32, name=f"bank{i}")
             nc.tensor.matmul_mx(
                 bank[:],
                 lhsT=query_codes[:].bitcast(FP8X4),
                 lhsT_scale=query_scales[:],
                 rhs=key_words[:, tokens].bitcast(FP8X4),
-                rhs_scale=key_scales[4 * j : P, :],
+                rhs_scale=key_scales[4 * j : P, tokens.start - j * N : tokens.stop - j * N],
                 start=True,
                 stop=True,
             )
-            if j % 2 == 0:
-                nc.scalar.copy(products[:, tokens], bank[:])
-            else:
-                nc.vector.tensor_copy(products[:, tokens], bank[:])
+            copy = nc.scalar.copy if i % 2 == 0 else nc.vector.tensor_copy
+            copy(products[:, tokens], bank[:])
 
         first = pool.tile([P, SLOTS], F32, name="first")
         second = pool.tile([P, SLOTS], F32, name="second")
+        old_listed = pool.tile([P, SLOTS], F32, name="old_listed")
         scores = pool.tile([P, SLOTS], F32, name="scores")
         weights = pool.tile([P, SLOTS], F32, name="weights")
-        nc.scalar.activation(second[:], products[:].indirect(list2[:]), ACT.Copy)
-        nc.vector.tensor_copy(first[:], products[:].indirect(list1[:]))
-        old_listed = pool.tile([P, SLOTS], F32, name="old_listed", tag="products_then_old_listed")
-        nc.scalar.activation(old_listed[:], old_table[:].indirect(list3[:]), ACT.Copy)
         halves = [slice(h * HALF, (h + 1) * HALF) for h in range(2)]
+
+        def entries(offsets, slots):
+            return offsets[:, slots.start // PER_COLUMN : slots.stop // PER_COLUMN]
+
+        for slots in halves:
+            nc.scalar.activation(second[:, slots], products[:].indirect(entries(list2, slots)), ACT.Copy)
+            nc.vector.tensor_copy(first[:, slots], products[:].indirect(entries(list1, slots)))
+        nc.scalar.activation(old_listed[:], old_table[:].indirect(list3[:]), ACT.Copy)
         for slots in halves:
             nc.vector.tensor_tensor(scores[:, slots], first[:, slots], second[:, slots], ALU.subtract)
         for slots in halves:

@@ -53,11 +53,11 @@ def tile_attend_difference_lean_timesold_heads_kernel(tc, query, keys_words, key
             nc.sync.dma_start(offsets[:], source)
             return offsets
 
-        list2 = load_list("list2", offs2)
-        list1 = load_list("list1", offs)
         old_table = pool.tile([P, T], F32, name="old_table")
         nc.sync.dma_start(old_table[:], old)
         list3 = load_list("list3", offs3)
+        list2 = load_list("list2", offs2)
+        list1 = load_list("list1", offs)
         list4 = load_list("list4", offs4)
         base_table = pool.tile([P, T], F32, name="base_table")
         nc.sync.dma_start(base_table[:], base)
@@ -76,7 +76,13 @@ def tile_attend_difference_lean_timesold_heads_kernel(tc, query, keys_words, key
         query_scales = pool.tile([P, Q], U8, name="query_scales", align_bytes=64)
         nc.vector.quantize_mx(query_codes[:].bitcast(FP8X4), query_scales[:], query_bf16[:].rearrange("p q j -> p (q j)"))
 
-        products = pool.tile([P, T], F32, name="products")
+        def entries(offsets, start, stop):
+            return offsets[:, start // PER_COLUMN : stop // PER_COLUMN]
+
+        old_early = pool.tile([P, HALF], F32, name="old_early")
+        nc.scalar.activation(old_early[:], old_table[:].indirect(entries(list3, 0, HALF)), ACT.Copy)
+
+        products = pool.tile([P, T], F32, name="products", tag="products_then_old_late")
         starts = [0, N, 2 * N, 3 * N, 3 * N + N // 2, T]
         for i in range(len(starts) - 1):
             tokens = slice(starts[i], starts[i + 1])
@@ -91,31 +97,39 @@ def tile_attend_difference_lean_timesold_heads_kernel(tc, query, keys_words, key
                 start=True,
                 stop=True,
             )
-            copy = nc.scalar.copy if i % 2 == 0 else nc.vector.tensor_copy
-            copy(products[:, tokens], bank[:])
+            nc.vector.tensor_copy(products[:, tokens], bank[:])
 
         first = pool.tile([P, SLOTS], F32, name="first")
         second = pool.tile([P, SLOTS], F32, name="second")
-        old_listed = pool.tile([P, SLOTS], F32, name="old_listed")
-        scores = pool.tile([P, SLOTS], F32, name="scores")
+        early, late = slice(0, HALF), slice(HALF, SLOTS)
+        nc.scalar.activation(second[:, early], products[:].indirect(entries(list2, 0, HALF)), ACT.Copy)
+        nc.vector.tensor_copy(first[:, early], products[:].indirect(entries(list1, 0, HALF)))
+        nc.scalar.activation(first[:, late], products[:].indirect(entries(list1, HALF, SLOTS)), ACT.Copy)
+        nc.scalar.activation(second[:, late], products[:].indirect(entries(list2, HALF, SLOTS)), ACT.Copy)
+        old_late = pool.tile([P, HALF], F32, name="old_late", tag="products_then_old_late")
+        nc.scalar.activation(old_late[:], old_table[:].indirect(entries(list3, HALF, SLOTS)), ACT.Copy)
+
+        scores = pool.tile([P, HALF], F32, name="scores")
         weights = pool.tile([P, SLOTS], F32, name="weights")
-        halves = [slice(h * HALF, (h + 1) * HALF) for h in range(2)]
-
-        def entries(offsets, slots):
-            return offsets[:, slots.start // PER_COLUMN : slots.stop // PER_COLUMN]
-
-        for slots in halves:
-            nc.scalar.activation(second[:, slots], products[:].indirect(entries(list2, slots)), ACT.Copy)
-            nc.vector.tensor_copy(first[:, slots], products[:].indirect(entries(list1, slots)))
-        nc.scalar.activation(old_listed[:], old_table[:].indirect(list3[:]), ACT.Copy)
-        for slots in halves:
+        pieces = [slice(0, HALF // 2), slice(HALF // 2, HALF)]
+        for slots in pieces:
             nc.vector.tensor_tensor(scores[:, slots], first[:, slots], second[:, slots], ALU.subtract)
-        for slots in halves:
+        for slots in pieces:
             nc.vector.tensor_scalar_max(weights[:, slots], scores[:, slots], 0.0)
-        nc.vector.tensor_tensor(placed[:].indirect(list4[:]), weights[:], old_listed[:], ALU.mult)
+
+        def place(slots, old_listed):
+            nc.vector.tensor_tensor(placed[:].indirect(entries(list4, slots.start, slots.stop)), weights[:, slots], old_listed, ALU.mult)
+
+        place(pieces[0], old_early[:, pieces[0]])
+        nc.vector.tensor_tensor(scores[:], first[:, late], second[:, late], ALU.subtract)
+        nc.scalar.activation(weights[:, late], scores[:], ACT.Relu)
+        place(pieces[1], old_early[:, pieces[1]])
+        place(late, old_late[:])
 
         result = pool.tile([P, T], F32, name="result")
-        for j, queue in enumerate((nc.sync, nc.scalar, nc.sync, nc.scalar)):
-            tokens = slice(j * N, (j + 1) * N)
+        cuts = [0, 128, 320, 512, 768, 1024]
+        for i in range(len(cuts) - 1):
+            tokens = slice(cuts[i], cuts[i + 1])
             nc.vector.tensor_tensor(result[:, tokens], placed[:, tokens], base_table[:, tokens], ALU.add)
+            queue = nc.sync if i % 2 == 0 else nc.scalar
             queue.dma_start(out[:, tokens], result[:, tokens])

@@ -35,6 +35,13 @@ def tile_attend_difference_lean_timesold_heads_kernel(tc, query, keys_words, key
         query_rows = pool.tile([P, PACK, Q], F32, name="query_rows")
         nc.sync.dma_start(query_rows[:], query.rearrange("(p j) q -> p j q", j=PACK))
 
+        key_words = pool.tile([P, T], U32, name="key_words", align_bytes=64)
+        word_rows = keys_words[0].rearrange("p n t -> p (n t)").bitcast(I32)
+
+        def load_words(start, stop):
+            nc.sync.dma_start(key_words[:].bitcast(I32)[:, start:stop], word_rows[:, start:stop])
+
+        load_words(0, T // 2)
         scale_rows = keys_scales[0].bitcast(I32)
         for quadrant in range(4):
             nc.sync.dma_start(
@@ -42,11 +49,7 @@ def tile_attend_difference_lean_timesold_heads_kernel(tc, query, keys_words, key
                 scale_rows[4 * quadrant : 4 * quadrant + 4, :].rearrange("r (j c) -> j r c", j=QUARTERS),
             )
 
-        key_words = pool.tile([P, T], U32, name="key_words", align_bytes=64)
-        word_rows = keys_words[0].rearrange("p n t -> p (n t)").bitcast(I32)
-        for h in range(2):
-            tokens = slice(h * T // 2, (h + 1) * T // 2)
-            nc.sync.dma_start(key_words[:].bitcast(I32)[:, tokens], word_rows[:, tokens])
+        load_words(T // 2, T)
 
         def load_list(name, source):
             offsets = pool.tile([P, SLOTS // PER_COLUMN], U16, name=name)
@@ -66,8 +69,7 @@ def tile_attend_difference_lean_timesold_heads_kernel(tc, query, keys_words, key
         nc.vector.memset(placed[:], 0.0)
 
         query_bf16 = pool.tile([P, Q, PACK], BF16, name="query_bf16", align_bytes=64)
-        for h, copy in enumerate((nc.vector.tensor_copy, nc.scalar.copy)):
-            rows = slice(h * Q // 2, (h + 1) * Q // 2)
+        for rows, copy in ((slice(0, 96), nc.vector.tensor_copy), (slice(96, Q), nc.scalar.copy)):
             copy(
                 query_bf16[:, rows, :].rearrange("p (c i) j -> p c j i", i=4),
                 query_rows[:, :, rows].rearrange("p j (c i) -> p c j i", i=4),
@@ -79,11 +81,8 @@ def tile_attend_difference_lean_timesold_heads_kernel(tc, query, keys_words, key
         def entries(offsets, start, stop):
             return offsets[:, start // PER_COLUMN : stop // PER_COLUMN]
 
-        old_early = pool.tile([P, HALF], F32, name="old_early")
-        nc.scalar.activation(old_early[:], old_table[:].indirect(entries(list3, 0, HALF)), ACT.Copy)
-
         products = pool.tile([P, T], F32, name="products", tag="products_then_old_late")
-        starts = [0, N, 2 * N, 3 * N, 3 * N + N // 2, T]
+        starts = [0, N, 2 * N, 2 * N + N // 2, 3 * N, 3 * N + N // 2, T]
         for i in range(len(starts) - 1):
             tokens = slice(starts[i], starts[i + 1])
             j = tokens.start // N
@@ -97,7 +96,11 @@ def tile_attend_difference_lean_timesold_heads_kernel(tc, query, keys_words, key
                 start=True,
                 stop=True,
             )
-            nc.vector.tensor_copy(products[:, tokens], bank[:])
+            copy = nc.scalar.copy if i < 2 else nc.vector.tensor_copy
+            copy(products[:, tokens], bank[:])
+
+        old_early = pool.tile([P, HALF], F32, name="old_early")
+        nc.scalar.activation(old_early[:], old_table[:].indirect(entries(list3, 0, HALF)), ACT.Copy)
 
         first = pool.tile([P, SLOTS], F32, name="first")
         second = pool.tile([P, SLOTS], F32, name="second")

from contextlib import ExitStack

import concourse.mybir as mybir

D, T, SLOTS, Q = 512, 1024, 512, 128
FLOPS = 2 * D * Q * T

F32 = mybir.dt.float32
BF16 = mybir.dt.bfloat16
I32 = mybir.dt.int32
U32 = mybir.dt.uint32
U16 = mybir.dt.uint16
U8 = mybir.dt.uint8
FP8X4 = mybir.dt.float8_e4m3fn_x4
ALU = mybir.AluOpType
ACT = mybir.ActivationFunctionType

P = 128
PACK = 4
QUARTERS = 4
N = T // QUARTERS
HALF = SLOTS // 2
PER_COLUMN = 16


def tile_attend_difference_lean_timesold_heads_kernel(tc, query, keys_words, keys_scales, old, base, offs, offs2, offs3, offs4, out):
    nc = tc.nc
    with ExitStack() as ctx:
        pool = ctx.enter_context(tc.tile_pool(name="pool", bufs=1))
        psum = ctx.enter_context(tc.psum_pool(name="psum", bufs=1))

        key_scales = pool.tile([P, N], U8, name="key_scales", align_bytes=64)
        nc.vector.memset(key_scales[:].bitcast(U32), 0)

        query_rows = pool.tile([P, PACK, Q], F32, name="query_rows")
        nc.sync.dma_start(query_rows[:], query.rearrange("(p j) q -> p j q", j=PACK))

        key_words = pool.tile([P, T], U32, name="key_words", align_bytes=64)
        word_rows = keys_words[0].rearrange("p n t -> p (n t)").bitcast(I32)

        def load_words(start, stop):
            nc.sync.dma_start(key_words[:].bitcast(I32)[:, start:stop], word_rows[:, start:stop])

        load_words(0, T // 2)
        scale_rows = keys_scales[0].bitcast(I32)
        for quadrant in range(4):
            nc.sync.dma_start(
                key_scales[:].bitcast(I32)[32 * quadrant : 32 * quadrant + 16, :],
                scale_rows[4 * quadrant : 4 * quadrant + 4, :].rearrange("r (j c) -> j r c", j=QUARTERS),
            )

        load_words(T // 2, T)

        def load_list(name, source):
            offsets = pool.tile([P, SLOTS // PER_COLUMN], U16, name=name)
            nc.sync.dma_start(offsets[:], source)
            return offsets

        old_table = pool.tile([P, T], F32, name="old_table")
        nc.sync.dma_start(old_table[:], old)
        list3 = load_list("list3", offs3)
        list2 = load_list("list2", offs2)
        list1 = load_list("list1", offs)
        list4 = load_list("list4", offs4)
        base_table = pool.tile([P, T], F32, name="base_table")
        nc.sync.dma_start(base_table[:], base)

        placed = pool.tile([P, T], F32, name="placed")
        nc.vector.memset(placed[:], 0.0)

        query_bf16 = pool.tile([P, Q, PACK], BF16, name="query_bf16", align_bytes=64)
        for rows, copy in ((slice(0, 96), nc.vector.tensor_copy), (slice(96, Q), nc.scalar.copy)):
            copy(
                query_bf16[:, rows, :].rearrange("p (c i) j -> p c j i", i=4),
                query_rows[:, :, rows].rearrange("p j (c i) -> p c j i", i=4),
            )
        query_codes = pool.tile([P, Q], U32, name="query_codes", align_bytes=64)
        query_scales = pool.tile([P, Q], U8, name="query_scales", align_bytes=64)
        nc.vector.quantize_mx(query_codes[:].bitcast(FP8X4), query_scales[:], query_bf16[:].rearrange("p q j -> p (q j)"))

        def entries(offsets, start, stop):
            return offsets[:, start // PER_COLUMN : stop // PER_COLUMN]

        products = pool.tile([P, T], F32, name="products", tag="products_then_old_late")
        starts = [0, N, 2 * N, 2 * N + N // 2, 3 * N, 3 * N + N // 2, T]
        for i in range(len(starts) - 1):
            tokens = slice(starts[i], starts[i + 1])
            j = tokens.start // N
            bank = psum.tile([P, tokens.stop - tokens.start], F32, name=f"bank{i}")
            nc.tensor.matmul_mx(
                bank[:],
                lhsT=query_codes[:].bitcast(FP8X4),
                lhsT_scale=query_scales[:],
                rhs=key_words[:, tokens].bitcast(FP8X4),
                rhs_scale=key_scales[4 * j : P, tokens.start - j * N : tokens.stop - j * N],
                start=True,
                stop=True,
            )
            copy = nc.scalar.copy if i < 2 else nc.vector.tensor_copy
            copy(products[:, tokens], bank[:])

        old_early = pool.tile([P, HALF], F32, name="old_early")
        nc.scalar.activation(old_early[:], old_table[:].indirect(entries(list3, 0, HALF)), ACT.Copy)

        first = pool.tile([P, SLOTS], F32, name="first")
        second = pool.tile([P, SLOTS], F32, name="second")
        early, late = slice(0, HALF), slice(HALF, SLOTS)
        nc.scalar.activation(second[:, early], products[:].indirect(entries(list2, 0, HALF)), ACT.Copy)
        nc.vector.tensor_copy(first[:, early], products[:].indirect(entries(list1, 0, HALF)))
        nc.scalar.activation(first[:, late], products[:].indirect(entries(list1, HALF, SLOTS)), ACT.Copy)
        nc.scalar.activation(second[:, late], products[:].indirect(entries(list2, HALF, SLOTS)), ACT.Copy)
        old_late = pool.tile([P, HALF], F32, name="old_late", tag="products_then_old_late")
        nc.scalar.activation(old_late[:], old_table[:].indirect(entries(list3, HALF, SLOTS)), ACT.Copy)

        scores = pool.tile([P, HALF], F32, name="scores")
        weights = pool.tile([P, SLOTS], F32, name="weights")
        pieces = [slice(0, HALF // 2), slice(HALF // 2, HALF)]
        for slots in pieces:
            nc.vector.tensor_tensor(scores[:, slots], first[:, slots], second[:, slots], ALU.subtract)
        for slots in pieces:
            nc.vector.tensor_scalar_max(weights[:, slots], scores[:, slots], 0.0)

        def place(slots, old_listed):
            nc.vector.tensor_tensor(placed[:].indirect(entries(list4, slots.start, slots.stop)), weights[:, slots], old_listed, ALU.mult)

        place(pieces[0], old_early[:, pieces[0]])
        nc.vector.tensor_tensor(scores[:], first[:, late], second[:, late], ALU.subtract)
        nc.scalar.activation(weights[:, late], scores[:], ACT.Relu)
        place(pieces[1], old_early[:, pieces[1]])
        place(late, old_late[:])

        result = pool.tile([P, T], F32, name="result")
        cuts = [0, 128, 320, 512, 768, 1024]
        for i in range(len(cuts) - 1):
            tokens = slice(cuts[i], cuts[i + 1])
            nc.vector.tensor_tensor(result[:, tokens], placed[:, tokens], base_table[:, tokens], ALU.add)
            queue = nc.sync if i % 2 == 0 else nc.scalar
            queue.dma_start(out[:, tokens], result[:, tokens])
